import numpy as np, ml_dtypes
CORES = [5,13,21,29,37,45,53,61,69,77,85,93,101,109,117,125]
N = 16
def setup_inputs(rng):
    return {"x": rng.standard_normal((N, 128, 2), dtype=np.float32).astype(ml_dtypes.bfloat16)}
def reference(x):
    g = np.concatenate(list(x), axis=1)
    return {"y": np.broadcast_to(g, (N,) + g.shape)}

@@ -1,0 +1,51 @@
+from concourse.bass import DstId, RemoteDMATransfer
+
+SCRATCH = {
+    "land": ("sbuf", [128, 32], "bfloat16"),
+    "relay": ("sbuf", [128, 2], "bfloat16"),
+}
+SEMAPHORES = ["loaded", "arrived", "sent", "stored"]
+
+RANK_CORE = 5
+HELPER = 6
+
+
+def dst_id(topo, core):
+    rid, pid, _se = topo.addr(core)
+    return DstId(rid=rid, pnc=pid)
+
+
+def rank_program(g, core, T, topo):
+    chip, k = divmod(core, 8)
+    rank = chip
+    cols = slice(2 * rank, 2 * rank + 2)
+    same = [c for c in range(16) if c != chip and (c & 1) == (chip & 1)]
+    other = [c for c in range(16) if (c & 1) != (chip & 1)]
+
+    if k == RANK_CORE:
+        g.dma_start(T.land[:, cols], T.x[:, :]).then_inc(T.sem.loaded, 16)
+        g.wait_ge(T.sem.loaded, 16)
+        g.remote_dma_fused(
+            [
+                RemoteDMATransfer(
+                    dst_ids=[dst_id(topo, chip * 8 + HELPER)], dma_engine_mask=0xFF00,
+                    remote_sem=T.sem.arrived, srcs=[T.land[:, cols]], dsts=[T.relay[:, :]]),
+                RemoteDMATransfer(
+                    dst_ids=[dst_id(topo, c * 8 + RANK_CORE) for c in same], dma_engine_mask=0x00FF,
+                    remote_sem=T.sem.arrived, srcs=[T.land[:, cols]], dsts=[T.land[:, cols] for c in same]),
+            ],
+            local_sem=T.sem.sent)
+        g.wait_ge(T.sem.arrived, 15 * 8)
+        g.dma_start(T.y[:, :], T.land[:, :]).then_inc(T.sem.stored, 16)
+        g.wait_ge(T.sem.sent, 16)
+        g.wait_ge(T.sem.stored, 16)
+    elif k == HELPER:
+        g.wait_ge(T.sem.arrived, 8)
+        g.remote_dma_fused(
+            [
+                RemoteDMATransfer(
+                    dst_ids=[dst_id(topo, c * 8 + RANK_CORE) for c in other], dma_engine_mask=0x00FF,
+                    remote_sem=T.sem.arrived, srcs=[T.relay[:, :]], dsts=[T.land[:, cols] for c in other]),
+            ],
+            local_sem=T.sem.sent)
+        g.wait_ge(T.sem.sent, 8)

@@ -2,12 +2,13 @@ from concourse.bass import DstId, RemoteDMATransfer
 
 SCRATCH = {
     "land": ("sbuf", [128, 32], "bfloat16"),
-    "relay": ("sbuf", [128, 2], "bfloat16"),
+    "stage": ("dram", [128, 2], "bfloat16"),
 }
-SEMAPHORES = ["loaded", "arrived", "sent", "stored"]
+SEMAPHORES = ["loaded", "own", "arrived", "sent", "stored"]
 
 RANK_CORE = 5
-HELPER = 6
+RELAYS = {6: (1, 3, 5, 7, 9, 11, 13, 15)}
+TO_RELAY_ENGINES = 8 // len(RELAYS)
 
 
 def dst_id(topo, core):
@@ -20,32 +21,34 @@ def rank_program(g, core, T, topo):
     rank = chip
     cols = slice(2 * rank, 2 * rank + 2)
     same = [c for c in range(16) if c != chip and (c & 1) == (chip & 1)]
-    other = [c for c in range(16) if (c & 1) != (chip & 1)]
 
     if k == RANK_CORE:
-        g.dma_start(T.land[:, cols], T.x[:, :]).then_inc(T.sem.loaded, 16)
+        g.dma_start(T.stage[:, :], T.x[:, :]).then_inc(T.sem.loaded, 16)
         g.wait_ge(T.sem.loaded, 16)
-        g.remote_dma_fused(
-            [
-                RemoteDMATransfer(
-                    dst_ids=[dst_id(topo, chip * 8 + HELPER)], dma_engine_mask=0xFF00,
-                    remote_sem=T.sem.arrived, srcs=[T.land[:, cols]], dsts=[T.relay[:, :]]),
-                RemoteDMATransfer(
-                    dst_ids=[dst_id(topo, c * 8 + RANK_CORE) for c in same], dma_engine_mask=0x00FF,
-                    remote_sem=T.sem.arrived, srcs=[T.land[:, cols]], dsts=[T.land[:, cols] for c in same]),
-            ],
-            local_sem=T.sem.sent)
+        e = TO_RELAY_ENGINES
+        transfers = [
+            RemoteDMATransfer(
+                dst_ids=[dst_id(topo, chip * 8 + h)], dma_engine_mask=((1 << e) - 1) << (8 + e * i),
+                remote_sem=T.sem.arrived, srcs=[T.stage[:, :]], dsts=[T.stage[:, :]])
+            for i, h in enumerate(RELAYS)
+        ]
+        transfers.append(RemoteDMATransfer(
+            dst_ids=[dst_id(topo, c * 8 + RANK_CORE) for c in same], dma_engine_mask=0x00FF,
+            remote_sem=T.sem.arrived, srcs=[T.stage[:, :]], dsts=[T.land[:, cols] for c in same]))
+        g.remote_dma_fused(transfers, local_sem=T.sem.sent)
+        g.dma_start(T.land[:, cols], T.x[:, :]).then_inc(T.sem.own, 16)
+        g.wait_ge(T.sem.own, 16)
         g.wait_ge(T.sem.arrived, 15 * 8)
         g.dma_start(T.y[:, :], T.land[:, :]).then_inc(T.sem.stored, 16)
         g.wait_ge(T.sem.sent, 16)
         g.wait_ge(T.sem.stored, 16)
-    elif k == HELPER:
-        g.wait_ge(T.sem.arrived, 8)
+    elif k in RELAYS:
+        g.wait_ge(T.sem.arrived, TO_RELAY_ENGINES)
         g.remote_dma_fused(
             [
                 RemoteDMATransfer(
-                    dst_ids=[dst_id(topo, c * 8 + RANK_CORE) for c in other], dma_engine_mask=0x00FF,
-                    remote_sem=T.sem.arrived, srcs=[T.relay[:, :]], dsts=[T.land[:, cols] for c in other]),
+                    dst_ids=[dst_id(topo, (chip ^ d) * 8 + RANK_CORE) for d in RELAYS[k]], dma_engine_mask=0x00FF,
+                    remote_sem=T.sem.arrived, srcs=[T.stage[:, :]], dsts=[T.land[:, cols] for d in RELAYS[k]]),
             ],
             local_sem=T.sem.sent)
         g.wait_ge(T.sem.sent, 8)

@@ -7,8 +7,7 @@ SCRATCH = {
 SEMAPHORES = ["loaded", "own", "arrived", "sent", "stored"]
 
 RANK_CORE = 5
-RELAYS = {6: (1, 3, 5, 7, 9, 11, 13, 15)}
-TO_RELAY_ENGINES = 8 // len(RELAYS)
+RELAYS = {6: (1, 3), 7: (5, 7), 2: (9, 11), 3: (13, 15)}
 
 
 def dst_id(topo, core):
@@ -25,25 +24,23 @@ def rank_program(g, core, T, topo):
     if k == RANK_CORE:
         g.dma_start(T.stage[:, :], T.x[:, :]).then_inc(T.sem.loaded, 16)
         g.wait_ge(T.sem.loaded, 16)
-        e = TO_RELAY_ENGINES
-        transfers = [
-            RemoteDMATransfer(
-                dst_ids=[dst_id(topo, chip * 8 + h)], dma_engine_mask=((1 << e) - 1) << (8 + e * i),
-                remote_sem=T.sem.arrived, srcs=[T.stage[:, :]], dsts=[T.stage[:, :]])
-            for i, h in enumerate(RELAYS)
-        ]
-        transfers.append(RemoteDMATransfer(
-            dst_ids=[dst_id(topo, c * 8 + RANK_CORE) for c in same], dma_engine_mask=0x00FF,
-            remote_sem=T.sem.arrived, srcs=[T.stage[:, :]], dsts=[T.land[:, cols] for c in same]))
-        g.remote_dma_fused(transfers, local_sem=T.sem.sent)
+        g.remote_dma_fused(
+            [
+                RemoteDMATransfer(
+                    dst_ids=[dst_id(topo, chip * 8 + h) for h in RELAYS]
+                    + [dst_id(topo, c * 8 + RANK_CORE) for c in same],
+                    dma_engine_mask=0x00FF, remote_sem=T.sem.arrived, srcs=[T.stage[:, :]],
+                    dsts=[T.stage[:, :] for h in RELAYS] + [T.land[:, cols] for c in same]),
+            ],
+            local_sem=T.sem.sent)
         g.dma_start(T.land[:, cols], T.x[:, :]).then_inc(T.sem.own, 16)
         g.wait_ge(T.sem.own, 16)
         g.wait_ge(T.sem.arrived, 15 * 8)
         g.dma_start(T.y[:, :], T.land[:, :]).then_inc(T.sem.stored, 16)
-        g.wait_ge(T.sem.sent, 16)
+        g.wait_ge(T.sem.sent, 8)
         g.wait_ge(T.sem.stored, 16)
     elif k in RELAYS:
-        g.wait_ge(T.sem.arrived, TO_RELAY_ENGINES)
+        g.wait_ge(T.sem.arrived, 8)
         g.remote_dma_fused(
             [
                 RemoteDMATransfer(

@@ -7,7 +7,8 @@ SCRATCH = {
 SEMAPHORES = ["loaded", "own", "arrived", "sent", "stored"]
 
 RANK_CORE = 5
-RELAYS = {6: (1, 3), 7: (5, 7), 2: (9, 11), 3: (13, 15)}
+RELAYS = {6: (1, 3), 7: (5, 7), 2: (9, 11), 3: (13, 15), 0: (2, 4), 1: (6, 8), 4: (10, 12)}
+DIRECT = (14,)
 
 
 def dst_id(topo, core):
@@ -19,7 +20,6 @@ def rank_program(g, core, T, topo):
     chip, k = divmod(core, 8)
     rank = chip
     cols = slice(2 * rank, 2 * rank + 2)
-    same = [c for c in range(16) if c != chip and (c & 1) == (chip & 1)]
 
     if k == RANK_CORE:
         g.dma_start(T.stage[:, :], T.x[:, :]).then_inc(T.sem.loaded, 16)
@@ -28,9 +28,9 @@ def rank_program(g, core, T, topo):
             [
                 RemoteDMATransfer(
                     dst_ids=[dst_id(topo, chip * 8 + h) for h in RELAYS]
-                    + [dst_id(topo, c * 8 + RANK_CORE) for c in same],
+                    + [dst_id(topo, (chip ^ d) * 8 + RANK_CORE) for d in DIRECT],
                     dma_engine_mask=0x00FF, remote_sem=T.sem.arrived, srcs=[T.stage[:, :]],
-                    dsts=[T.stage[:, :] for h in RELAYS] + [T.land[:, cols] for c in same]),
+                    dsts=[T.stage[:, :] for h in RELAYS] + [T.land[:, cols] for d in DIRECT]),
             ],
             local_sem=T.sem.sent)
         g.dma_start(T.land[:, cols], T.x[:, :]).then_inc(T.sem.own, 16)

@@ -4,11 +4,11 @@ SCRATCH = {
     "land": ("sbuf", [128, 32], "bfloat16"),
     "stage": ("dram", [128, 2], "bfloat16"),
 }
-SEMAPHORES = ["loaded", "own", "arrived", "sent", "stored"]
+SEMAPHORES = ["loaded", "arrived", "sent", "stored"]
 
 RANK_CORE = 5
-RELAYS = {6: (1, 3), 7: (5, 7), 2: (9, 11), 3: (13, 15), 0: (2, 4), 1: (6, 8), 4: (10, 12)}
-DIRECT = (14,)
+RELAYS = {6: (3, 1), 7: (5, 7), 2: (9, 11), 3: (13, 15), 0: (2, 4), 4: (10, 12), 1: (6, 0)}
+DIRECT = (8, 14)
 
 
 def dst_id(topo, core):
@@ -33,9 +33,7 @@ def rank_program(g, core, T, topo):
                     dsts=[T.stage[:, :] for h in RELAYS] + [T.land[:, cols] for d in DIRECT]),
             ],
             local_sem=T.sem.sent)
-        g.dma_start(T.land[:, cols], T.x[:, :]).then_inc(T.sem.own, 16)
-        g.wait_ge(T.sem.own, 16)
-        g.wait_ge(T.sem.arrived, 15 * 8)
+        g.wait_ge(T.sem.arrived, 16 * 8)
         g.dma_start(T.y[:, :], T.land[:, :]).then_inc(T.sem.stored, 16)
         g.wait_ge(T.sem.sent, 8)
         g.wait_ge(T.sem.stored, 16)

from concourse.bass import DstId, RemoteDMATransfer

SCRATCH = {
    "land": ("sbuf", [128, 32], "bfloat16"),
    "stage": ("dram", [128, 2], "bfloat16"),
}
SEMAPHORES = ["loaded", "arrived", "sent", "stored"]

RANK_CORE = 5
RELAYS = {6: (3, 1), 7: (5, 7), 2: (9, 11), 3: (13, 15), 0: (2, 4), 4: (10, 12), 1: (6, 0)}
DIRECT = (8, 14)


def dst_id(topo, core):
    rid, pid, _se = topo.addr(core)
    return DstId(rid=rid, pnc=pid)


def rank_program(g, core, T, topo):
    chip, k = divmod(core, 8)
    rank = chip
    cols = slice(2 * rank, 2 * rank + 2)

    if k == RANK_CORE:
        g.dma_start(T.stage[:, :], T.x[:, :]).then_inc(T.sem.loaded, 16)
        g.wait_ge(T.sem.loaded, 16)
        g.remote_dma_fused(
            [
                RemoteDMATransfer(
                    dst_ids=[dst_id(topo, chip * 8 + h) for h in RELAYS]
                    + [dst_id(topo, (chip ^ d) * 8 + RANK_CORE) for d in DIRECT],
                    dma_engine_mask=0x00FF, remote_sem=T.sem.arrived, srcs=[T.stage[:, :]],
                    dsts=[T.stage[:, :] for h in RELAYS] + [T.land[:, cols] for d in DIRECT]),
            ],
            local_sem=T.sem.sent)
        g.wait_ge(T.sem.arrived, 16 * 8)
        g.dma_start(T.y[:, :], T.land[:, :]).then_inc(T.sem.stored, 16)
        g.wait_ge(T.sem.sent, 8)
        g.wait_ge(T.sem.stored, 16)
    elif k in RELAYS:
        g.wait_ge(T.sem.arrived, 8)
        g.remote_dma_fused(
            [
                RemoteDMATransfer(
                    dst_ids=[dst_id(topo, (chip ^ d) * 8 + RANK_CORE) for d in RELAYS[k]], dma_engine_mask=0x00FF,
                    remote_sem=T.sem.arrived, srcs=[T.stage[:, :]], dsts=[T.land[:, cols] for d in RELAYS[k]]),
            ],
            local_sem=T.sem.sent)
        g.wait_ge(T.sem.sent, 8)
